import numpy as np
import ml_dtypes

BF16 = ml_dtypes.bfloat16


def bf(x):
    return np.asarray(x, np.float32).astype(BF16)


def f32(x):
    return np.asarray(x, np.float32)


def f64(x):
    return np.asarray(x).astype(np.float64)


def striped(idx):
    return np.tile(idx.reshape(-1, 16).T, (8, 1))


S, K, M, N, D, V = 512, 128, 256, 384, 3, 128


def setup_inputs():
    return {"table": bf(np.random.standard_normal((K, S))), "w": bf(np.random.standard_normal((D, K, M)) / np.sqrt(D * K)), "r": f32(np.random.standard_normal((M, V))), "offs": striped(np.random.permutation(np.tile(np.arange(S), 2))[:N])}


def reference(table, w, r, offs):
    idx = offs[:16].T.reshape(-1)
    x = f64(table)[:, idx]
    y = sum(f64(w)[t].T @ x[:, t * V : (t + 1) * V] for t in range(D))
    return y + f64(r)

@@ -1,0 +1,45 @@
+import concourse.mybir as mybir
+
+BF16, F32, U16 = mybir.dt.bfloat16, mybir.dt.float32, mybir.dt.uint16
+ADD = mybir.AluOpType.add
+
+P = 128
+S = 512
+T = 3
+V = 128
+M = 256
+BLOCKS = M // P
+PIECE_COLS = V // 16
+
+FLOPS = 2 * P * M * T * V
+
+
+def tile_gather_matmul_kernel(tc, table, w, r, offs, out):
+    nc = tc.nc
+    with (
+        tc.tile_pool(name="held", bufs=1) as held,
+        tc.psum_pool(name="psum", bufs=1) as psum,
+    ):
+        offsets = held.tile([P, T * PIECE_COLS], U16, name="offsets")
+        nc.sync.dma_start(offsets[:], offs)
+        nodes = held.tile([P, S], BF16, name="nodes")
+        nc.scalar.dma_start(nodes[:], table)
+        weights = held.tile([P, T, M], BF16, name="weights")
+        nc.sync.dma_start(weights[:], w.rearrange("t k m -> k t m"))
+        own = held.tile([P, BLOCKS, V], F32, name="own")
+        nc.gpsimd.dma_start(own[:], r.rearrange("(a p) v -> p a v", p=P))
+
+        for a in range(BLOCKS):
+            bank = psum.tile([P, V], F32, name=f"bank{a}")
+            for t in range(T):
+                nc.tensor.matmul(
+                    bank[:],
+                    weights[:, t, a * P : (a + 1) * P],
+                    nodes[:].indirect(offsets[:, t * PIECE_COLS : (t + 1) * PIECE_COLS]),
+                    start=(t == 0),
+                    stop=(t == T - 1),
+                )
+            result = held.tile([P, V], F32, name=f"result{a}")
+            nc.vector.tensor_tensor(result[:], bank[:], own[:, a, :], ADD)
+            store_queue = nc.sync if a % 2 == 0 else nc.scalar
+            store_queue.dma_start(out[a * P : (a + 1) * P, :], result[:])

@@ -11,6 +11,9 @@ M = 256
 BLOCKS = M // P
 PIECE_COLS = V // 16
 
+WARM_COLS = 512
+WARM_MATMULS = 3
+
 FLOPS = 2 * P * M * T * V
 
 
@@ -28,6 +31,12 @@ def tile_gather_matmul_kernel(tc, table, w, r, offs, out):
         nc.sync.dma_start(weights[:], w.rearrange("t k m -> k t m"))
         own = held.tile([P, BLOCKS, V], F32, name="own")
         nc.gpsimd.dma_start(own[:], r.rearrange("(a p) v -> p a v", p=P))
+
+        zeros = held.tile([P, WARM_COLS], BF16, name="zeros")
+        nc.vector.memset(zeros[:], 0.0)
+        unused = psum.tile([P, WARM_COLS], F32, name="unused")
+        for i in range(WARM_MATMULS):
+            nc.tensor.matmul(unused[:], zeros[:, 0:P], zeros[:], start=True, stop=True)
 
         for a in range(BLOCKS):
             bank = psum.tile([P, V], F32, name=f"bank{a}")

@@ -11,9 +11,6 @@ M = 256
 BLOCKS = M // P
 PIECE_COLS = V // 16
 
-WARM_COLS = 512
-WARM_MATMULS = 3
-
 FLOPS = 2 * P * M * T * V
 
 
@@ -30,13 +27,7 @@ def tile_gather_matmul_kernel(tc, table, w, r, offs, out):
         weights = held.tile([P, T, M], BF16, name="weights")
         nc.sync.dma_start(weights[:], w.rearrange("t k m -> k t m"))
         own = held.tile([P, BLOCKS, V], F32, name="own")
-        nc.gpsimd.dma_start(own[:], r.rearrange("(a p) v -> p a v", p=P))
-
-        zeros = held.tile([P, WARM_COLS], BF16, name="zeros")
-        nc.vector.memset(zeros[:], 0.0)
-        unused = psum.tile([P, WARM_COLS], F32, name="unused")
-        for i in range(WARM_MATMULS):
-            nc.tensor.matmul(unused[:], zeros[:, 0:P], zeros[:], start=True, stop=True)
+        nc.scalar.dma_start(own[:], r.rearrange("(a p) v -> p a v", p=P))
 
         for a in range(BLOCKS):
             bank = psum.tile([P, V], F32, name=f"bank{a}")

@@ -24,22 +24,25 @@ def tile_gather_matmul_kernel(tc, table, w, r, offs, out):
         nc.sync.dma_start(offsets[:], offs)
         nodes = held.tile([P, S], BF16, name="nodes")
         nc.scalar.dma_start(nodes[:], table)
-        weights = held.tile([P, T, M], BF16, name="weights")
-        nc.sync.dma_start(weights[:], w.rearrange("t k m -> k t m"))
+        weights = [held.tile([P, M], BF16, name=f"weights{t}") for t in range(T)]
+        for t in range(T):
+            nc.sync.dma_start(weights[t][:], w[t])
         own = held.tile([P, BLOCKS, V], F32, name="own")
         nc.scalar.dma_start(own[:], r.rearrange("(a p) v -> p a v", p=P))
 
-        for a in range(BLOCKS):
-            bank = psum.tile([P, V], F32, name=f"bank{a}")
-            for t in range(T):
+        banks = [psum.tile([P, V], F32, name=f"bank{a}") for a in range(BLOCKS)]
+        for t in range(T):
+            for a in range(BLOCKS):
                 nc.tensor.matmul(
-                    bank[:],
-                    weights[:, t, a * P : (a + 1) * P],
+                    banks[a][:],
+                    weights[t][:, a * P : (a + 1) * P],
                     nodes[:].indirect(offsets[:, t * PIECE_COLS : (t + 1) * PIECE_COLS]),
                     start=(t == 0),
                     stop=(t == T - 1),
                 )
+
+        for a in range(BLOCKS):
             result = held.tile([P, V], F32, name=f"result{a}")
-            nc.vector.tensor_tensor(result[:], bank[:], own[:, a, :], ADD)
+            nc.vector.tensor_tensor(result[:], banks[a][:], own[:, a, :], ADD)
             store_queue = nc.sync if a % 2 == 0 else nc.scalar
             store_queue.dma_start(out[a * P : (a + 1) * P, :], result[:])

@@ -25,8 +25,9 @@ def tile_gather_matmul_kernel(tc, table, w, r, offs, out):
         nodes = held.tile([P, S], BF16, name="nodes")
         nc.scalar.dma_start(nodes[:], table)
         weights = [held.tile([P, M], BF16, name=f"weights{t}") for t in range(T)]
-        for t in range(T):
-            nc.sync.dma_start(weights[t][:], w[t])
+        nc.sync.dma_start(weights[0][:], w[0])
+        for t in range(1, T):
+            nc.scalar.dma_start(weights[t][:], w[t])
         own = held.tile([P, BLOCKS, V], F32, name="own")
         nc.scalar.dma_start(own[:], r.rearrange("(a p) v -> p a v", p=P))
 

@@ -10,6 +10,7 @@ V = 128
 M = 256
 BLOCKS = M // P
 PIECE_COLS = V // 16
+ROW_ALIGN = 256
 
 FLOPS = 2 * P * M * T * V
 
@@ -20,15 +21,15 @@ def tile_gather_matmul_kernel(tc, table, w, r, offs, out):
         tc.tile_pool(name="held", bufs=1) as held,
         tc.psum_pool(name="psum", bufs=1) as psum,
     ):
-        offsets = held.tile([P, T * PIECE_COLS], U16, name="offsets")
+        offsets = held.tile([P, T * PIECE_COLS], U16, name="offsets", align_bytes=ROW_ALIGN)
         nc.sync.dma_start(offsets[:], offs)
-        nodes = held.tile([P, S], BF16, name="nodes")
+        nodes = held.tile([P, S], BF16, name="nodes", align_bytes=ROW_ALIGN)
         nc.scalar.dma_start(nodes[:], table)
-        weights = [held.tile([P, M], BF16, name=f"weights{t}") for t in range(T)]
+        weights = [held.tile([P, M], BF16, name=f"weights{t}", align_bytes=ROW_ALIGN) for t in range(T)]
         nc.sync.dma_start(weights[0][:], w[0])
         for t in range(1, T):
             nc.scalar.dma_start(weights[t][:], w[t])
-        own = held.tile([P, BLOCKS, V], F32, name="own")
+        own = held.tile([P, BLOCKS, V], F32, name="own", align_bytes=ROW_ALIGN)
         nc.scalar.dma_start(own[:], r.rearrange("(a p) v -> p a v", p=P))
 
         banks = [psum.tile([P, V], F32, name=f"bank{a}") for a in range(BLOCKS)]
@@ -43,7 +44,7 @@ def tile_gather_matmul_kernel(tc, table, w, r, offs, out):
                 )
 
         for a in range(BLOCKS):
-            result = held.tile([P, V], F32, name=f"result{a}")
+            result = held.tile([P, V], F32, name=f"result{a}", align_bytes=ROW_ALIGN)
             nc.vector.tensor_tensor(result[:], banks[a][:], own[:, a, :], ADD)
             store_queue = nc.sync if a % 2 == 0 else nc.scalar
             store_queue.dma_start(out[a * P : (a + 1) * P, :], result[:])

@@ -46,5 +46,4 @@ def tile_gather_matmul_kernel(tc, table, w, r, offs, out):
         for a in range(BLOCKS):
             result = held.tile([P, V], F32, name=f"result{a}", align_bytes=ROW_ALIGN)
             nc.vector.tensor_tensor(result[:], banks[a][:], own[:, a, :], ADD)
-            store_queue = nc.sync if a % 2 == 0 else nc.scalar
-            store_queue.dma_start(out[a * P : (a + 1) * P, :], result[:])
+            nc.sync.dma_start(out[a * P : (a + 1) * P, :], result[:])

@@ -21,16 +21,15 @@ def tile_gather_matmul_kernel(tc, table, w, r, offs, out):
         tc.tile_pool(name="held", bufs=1) as held,
         tc.psum_pool(name="psum", bufs=1) as psum,
     ):
+        nodes = held.tile([P, S], BF16, name="nodes", align_bytes=ROW_ALIGN)
+        nc.sync.dma_start(nodes[:], table)
         offsets = held.tile([P, T * PIECE_COLS], U16, name="offsets", align_bytes=ROW_ALIGN)
         nc.sync.dma_start(offsets[:], offs)
-        nodes = held.tile([P, S], BF16, name="nodes", align_bytes=ROW_ALIGN)
-        nc.scalar.dma_start(nodes[:], table)
         weights = [held.tile([P, M], BF16, name=f"weights{t}", align_bytes=ROW_ALIGN) for t in range(T)]
-        nc.sync.dma_start(weights[0][:], w[0])
-        for t in range(1, T):
-            nc.scalar.dma_start(weights[t][:], w[t])
+        for t in range(T):
+            nc.sync.dma_start(weights[t][:], w[t])
         own = held.tile([P, BLOCKS, V], F32, name="own", align_bytes=ROW_ALIGN)
-        nc.scalar.dma_start(own[:], r.rearrange("(a p) v -> p a v", p=P))
+        nc.sync.dma_start(own[:], r.rearrange("(a p) v -> p a v", p=P))
 
         banks = [psum.tile([P, V], F32, name=f"bank{a}") for a in range(BLOCKS)]
         for t in range(T):

@@ -10,6 +10,8 @@ V = 128
 M = 256
 BLOCKS = M // P
 PIECE_COLS = V // 16
+BANK_COLS = 512
+WARM_UPS = 2
 ROW_ALIGN = 256
 
 FLOPS = 2 * P * M * T * V
@@ -30,6 +32,12 @@ def tile_gather_matmul_kernel(tc, table, w, r, offs, out):
             nc.sync.dma_start(weights[t][:], w[t])
         own = held.tile([P, BLOCKS, V], F32, name="own", align_bytes=ROW_ALIGN)
         nc.sync.dma_start(own[:], r.rearrange("(a p) v -> p a v", p=P))
+
+        zeros = held.tile([P, BANK_COLS], BF16, name="zeros", align_bytes=ROW_ALIGN)
+        nc.vector.memset(zeros[:], 0.0)
+        spare_bank = psum.tile([P, BANK_COLS], F32, name="spare_bank")
+        for warm in range(WARM_UPS):
+            nc.tensor.matmul(spare_bank[:], zeros[:, 0:P], zeros[:], start=True, stop=True)
 
         banks = [psum.tile([P, V], F32, name=f"bank{a}") for a in range(BLOCKS)]
         for t in range(T):

@@ -27,11 +27,13 @@ def tile_gather_matmul_kernel(tc, table, w, r, offs, out):
         nc.sync.dma_start(nodes[:], table)
         offsets = held.tile([P, T * PIECE_COLS], U16, name="offsets", align_bytes=ROW_ALIGN)
         nc.sync.dma_start(offsets[:], offs)
-        weights = [held.tile([P, M], BF16, name=f"weights{t}", align_bytes=ROW_ALIGN) for t in range(T)]
-        for t in range(T):
-            nc.sync.dma_start(weights[t][:], w[t])
-        own = held.tile([P, BLOCKS, V], F32, name="own", align_bytes=ROW_ALIGN)
-        nc.sync.dma_start(own[:], r.rearrange("(a p) v -> p a v", p=P))
+        first_weights = held.tile([P, M], BF16, name="first_weights", align_bytes=ROW_ALIGN)
+        nc.sync.dma_start(first_weights[:], w[0])
+        other_weights = held.tile([P, T - 1, M], BF16, name="other_weights", align_bytes=ROW_ALIGN)
+        nc.sync.dma_start(other_weights[:], w[1:T].rearrange("t k m -> k t m"))
+        own = [held.tile([P, V], F32, name=f"own{a}", align_bytes=ROW_ALIGN) for a in range(BLOCKS)]
+        for a in range(BLOCKS):
+            nc.sync.dma_start(own[a][:], r[a * P : (a + 1) * P, :])
 
         zeros = held.tile([P, BANK_COLS], BF16, name="zeros", align_bytes=ROW_ALIGN)
         nc.vector.memset(zeros[:], 0.0)
@@ -40,17 +42,23 @@ def tile_gather_matmul_kernel(tc, table, w, r, offs, out):
             nc.tensor.matmul(spare_bank[:], zeros[:, 0:P], zeros[:], start=True, stop=True)
 
         banks = [psum.tile([P, V], F32, name=f"bank{a}") for a in range(BLOCKS)]
-        for t in range(T):
-            for a in range(BLOCKS):
-                nc.tensor.matmul(
-                    banks[a][:],
-                    weights[t][:, a * P : (a + 1) * P],
-                    nodes[:].indirect(offsets[:, t * PIECE_COLS : (t + 1) * PIECE_COLS]),
-                    start=(t == 0),
-                    stop=(t == T - 1),
-                )
+
+        def gather_matmul(a, t, weights):
+            nc.tensor.matmul(
+                banks[a][:],
+                weights[:, a * P : (a + 1) * P],
+                nodes[:].indirect(offsets[:, t * PIECE_COLS : (t + 1) * PIECE_COLS]),
+                start=(t == 0),
+                stop=(t == T - 1),
+            )
+
+        for a in range(BLOCKS):
+            gather_matmul(a, 0, first_weights)
+        for a in range(BLOCKS):
+            for t in range(1, T):
+                gather_matmul(a, t, other_weights[:, t - 1, :])
 
         for a in range(BLOCKS):
             result = held.tile([P, V], F32, name=f"result{a}", align_bytes=ROW_ALIGN)
-            nc.vector.tensor_tensor(result[:], banks[a][:], own[:, a, :], ADD)
+            nc.vector.tensor_tensor(result[:], banks[a][:], own[a][:], ADD)
             nc.sync.dma_start(out[a * P : (a + 1) * P, :], result[:])

@@ -27,13 +27,14 @@ def tile_gather_matmul_kernel(tc, table, w, r, offs, out):
         nc.sync.dma_start(nodes[:], table)
         offsets = held.tile([P, T * PIECE_COLS], U16, name="offsets", align_bytes=ROW_ALIGN)
         nc.sync.dma_start(offsets[:], offs)
-        first_weights = held.tile([P, M], BF16, name="first_weights", align_bytes=ROW_ALIGN)
-        nc.sync.dma_start(first_weights[:], w[0])
-        other_weights = held.tile([P, T - 1, M], BF16, name="other_weights", align_bytes=ROW_ALIGN)
-        nc.sync.dma_start(other_weights[:], w[1:T].rearrange("t k m -> k t m"))
-        own = [held.tile([P, V], F32, name=f"own{a}", align_bytes=ROW_ALIGN) for a in range(BLOCKS)]
-        for a in range(BLOCKS):
-            nc.sync.dma_start(own[a][:], r[a * P : (a + 1) * P, :])
+        opening_weights = held.tile([P, P], BF16, name="opening_weights", align_bytes=ROW_ALIGN)
+        nc.sync.dma_start(opening_weights[:], w[0, :, 0:P])
+        closing_weights = held.tile([P, T - 1, P], BF16, name="closing_weights", align_bytes=ROW_ALIGN)
+        nc.sync.dma_start(closing_weights[:], w[1:T, :, 0:P].rearrange("t k m -> k t m"))
+        second_weights = held.tile([P, T, P], BF16, name="second_weights", align_bytes=ROW_ALIGN)
+        nc.sync.dma_start(second_weights[:], w[:, :, P:M].rearrange("t k m -> k t m"))
+        own = held.tile([P, BLOCKS, V], F32, name="own", align_bytes=ROW_ALIGN)
+        nc.sync.dma_start(own[:], r.rearrange("(a p) v -> p a v", p=P))
 
         zeros = held.tile([P, BANK_COLS], BF16, name="zeros", align_bytes=ROW_ALIGN)
         nc.vector.memset(zeros[:], 0.0)
@@ -42,23 +43,21 @@ def tile_gather_matmul_kernel(tc, table, w, r, offs, out):
             nc.tensor.matmul(spare_bank[:], zeros[:, 0:P], zeros[:], start=True, stop=True)
 
         banks = [psum.tile([P, V], F32, name=f"bank{a}") for a in range(BLOCKS)]
-
-        def gather_matmul(a, t, weights):
-            nc.tensor.matmul(
-                banks[a][:],
-                weights[:, a * P : (a + 1) * P],
-                nodes[:].indirect(offsets[:, t * PIECE_COLS : (t + 1) * PIECE_COLS]),
-                start=(t == 0),
-                stop=(t == T - 1),
-            )
-
+        weights = [
+            [opening_weights[:]] + [closing_weights[:, t - 1, :] for t in range(1, T)],
+            [second_weights[:, t, :] for t in range(T)],
+        ]
         for a in range(BLOCKS):
-            gather_matmul(a, 0, first_weights)
-        for a in range(BLOCKS):
-            for t in range(1, T):
-                gather_matmul(a, t, other_weights[:, t - 1, :])
+            for t in range(T):
+                nc.tensor.matmul(
+                    banks[a][:],
+                    weights[a][t],
+                    nodes[:].indirect(offsets[:, t * PIECE_COLS : (t + 1) * PIECE_COLS]),
+                    start=(t == 0),
+                    stop=(t == T - 1),
+                )
 
         for a in range(BLOCKS):
             result = held.tile([P, V], F32, name=f"result{a}", align_bytes=ROW_ALIGN)
-            nc.vector.tensor_tensor(result[:], banks[a][:], own[a][:], ADD)
+            nc.vector.tensor_tensor(result[:], banks[a][:], own[:, a, :], ADD)
             nc.sync.dma_start(out[a * P : (a + 1) * P, :], result[:])

@@ -10,8 +10,6 @@ V = 128
 M = 256
 BLOCKS = M // P
 PIECE_COLS = V // 16
-BANK_COLS = 512
-WARM_UPS = 2
 ROW_ALIGN = 256
 
 FLOPS = 2 * P * M * T * V
@@ -35,12 +33,6 @@ def tile_gather_matmul_kernel(tc, table, w, r, offs, out):
         nc.sync.dma_start(second_weights[:], w[:, :, P:M].rearrange("t k m -> k t m"))
         own = held.tile([P, BLOCKS, V], F32, name="own", align_bytes=ROW_ALIGN)
         nc.sync.dma_start(own[:], r.rearrange("(a p) v -> p a v", p=P))
-
-        zeros = held.tile([P, BANK_COLS], BF16, name="zeros", align_bytes=ROW_ALIGN)
-        nc.vector.memset(zeros[:], 0.0)
-        spare_bank = psum.tile([P, BANK_COLS], F32, name="spare_bank")
-        for warm in range(WARM_UPS):
-            nc.tensor.matmul(spare_bank[:], zeros[:, 0:P], zeros[:], start=True, stop=True)
 
         banks = [psum.tile([P, V], F32, name=f"bank{a}") for a in range(BLOCKS)]
         weights = [

import concourse.mybir as mybir

BF16, F32, U16 = mybir.dt.bfloat16, mybir.dt.float32, mybir.dt.uint16
ADD = mybir.AluOpType.add

P = 128
S = 512
T = 3
V = 128
M = 256
BLOCKS = M // P
PIECE_COLS = V // 16
ROW_ALIGN = 256

FLOPS = 2 * P * M * T * V


def tile_gather_matmul_kernel(tc, table, w, r, offs, out):
    nc = tc.nc
    with (
        tc.tile_pool(name="held", bufs=1) as held,
        tc.psum_pool(name="psum", bufs=1) as psum,
    ):
        nodes = held.tile([P, S], BF16, name="nodes", align_bytes=ROW_ALIGN)
        nc.sync.dma_start(nodes[:], table)
        offsets = held.tile([P, T * PIECE_COLS], U16, name="offsets", align_bytes=ROW_ALIGN)
        nc.sync.dma_start(offsets[:], offs)
        opening_weights = held.tile([P, P], BF16, name="opening_weights", align_bytes=ROW_ALIGN)
        nc.sync.dma_start(opening_weights[:], w[0, :, 0:P])
        closing_weights = held.tile([P, T - 1, P], BF16, name="closing_weights", align_bytes=ROW_ALIGN)
        nc.sync.dma_start(closing_weights[:], w[1:T, :, 0:P].rearrange("t k m -> k t m"))
        second_weights = held.tile([P, T, P], BF16, name="second_weights", align_bytes=ROW_ALIGN)
        nc.sync.dma_start(second_weights[:], w[:, :, P:M].rearrange("t k m -> k t m"))
        own = held.tile([P, BLOCKS, V], F32, name="own", align_bytes=ROW_ALIGN)
        nc.sync.dma_start(own[:], r.rearrange("(a p) v -> p a v", p=P))

        banks = [psum.tile([P, V], F32, name=f"bank{a}") for a in range(BLOCKS)]
        weights = [
            [opening_weights[:]] + [closing_weights[:, t - 1, :] for t in range(1, T)],
            [second_weights[:, t, :] for t in range(T)],
        ]
        for a in range(BLOCKS):
            for t in range(T):
                nc.tensor.matmul(
                    banks[a][:],
                    weights[a][t],
                    nodes[:].indirect(offsets[:, t * PIECE_COLS : (t + 1) * PIECE_COLS]),
                    start=(t == 0),
                    stop=(t == T - 1),
                )

        for a in range(BLOCKS):
            result = held.tile([P, V], F32, name=f"result{a}", align_bytes=ROW_ALIGN)
            nc.vector.tensor_tensor(result[:], banks[a][:], own[:, a, :], ADD)
            nc.sync.dma_start(out[a * P : (a + 1) * P, :], result[:])
